import numpy as np
import ml_dtypes


def mxq(x, axis, fmt="e4m3"):
    dtype, down = {"e4m3": (ml_dtypes.float8_e4m3fn, 7), "e5m2": (ml_dtypes.float8_e5m2, 14)}[fmt]
    v = np.moveaxis(np.asarray(x, np.float32).astype(ml_dtypes.bfloat16).astype(np.float64), axis, -1)
    blocks = v.reshape(v.shape[:-1] + (-1, 32))
    amax = np.abs(blocks).max(-1, keepdims=True)
    byte = np.maximum(np.where(amax > 0, np.frexp(amax)[1] - 1 + 127, 0) - down, 1)
    scale = np.exp2(byte - 127.0)
    codes = (blocks / scale).astype(np.float32).astype(dtype).astype(np.float64)
    return np.moveaxis((codes * scale).reshape(v.shape), -1, axis)


WIDE = False


def mx_kscale(k):
    if not WIDE:
        return np.ones(k)
    levels = np.array([10, -10, 5, -5, 0])
    if k % 512:
        return np.exp2(np.random.permutation(np.resize(levels, k // 32))).repeat(32)
    a = np.empty((k // 512, 16))
    for p in range(k // 512):
        a[p, :8] = np.random.permutation(np.resize(levels, 8))
        for g in range(8):
            far = levels[np.abs(levels - a[p, g]) >= 10]
            a[p, g + 8] = far[np.random.randint(len(far))]
    return np.exp2(a.ravel()).repeat(32)


def f64(x):
    return np.asarray(x).astype(np.float64)


def striped(idx):
    return np.tile(idx.reshape(-1, 16).T, (8, 1)).astype(np.uint16)


def unstriped(offs):
    return offs[:16].T.reshape(-1).astype(np.int64)


E2M1 = np.array([0.0, 0.5, 1.0, 1.5, 2.0, 3.0, 4.0, 6.0, -0.0, -0.5, -1.0, -1.5, -2.0, -3.0, -4.0, -6.0])


def pack_weight(w, fmt):
    k, n = w.shape
    w = f64(np.asarray(w, np.float32).astype(ml_dtypes.bfloat16)).reshape(k // 32, 32, n)
    amax = np.abs(w).max(1)
    if fmt == "e4m3":
        byte = np.frexp(amax)[1] - 1 + 127 - 7
    else:
        mant, ex = np.frexp(amax / 6.0)
        byte = np.where(mant > 0.5, ex, ex - 1) + 127
    byte = np.clip(np.where(amax > 0, byte, 1), 1, 254)
    scaled = (w * np.exp2(127.0 - byte)[:, None, :]).reshape(k, n).astype(np.float32)
    by_word = np.ascontiguousarray(scaled.reshape(k // 512, 128, 4, n).transpose(0, 1, 3, 2))
    if fmt == "e4m3":
        words = by_word.astype(ml_dtypes.float8_e4m3fn).view(np.uint8)
    else:
        c = by_word.astype(ml_dtypes.float4_e2m1fn).view(np.uint8) & 0xF
        words = (c[..., 0::2] | (c[..., 1::2] << 4)).reshape(k // 512, 128, 2 * n)
    return np.ascontiguousarray(words), np.ascontiguousarray(byte.astype(np.uint8).reshape(k // 512, 16, n))


def unpack_weight(words, scales, fmt):
    g, _, n = scales.shape
    words = np.ascontiguousarray(words).reshape(g, 128, n, -1)
    if fmt == "e4m3":
        vals = words.view(ml_dtypes.float8_e4m3fn).astype(np.float64)
    else:
        nib = np.empty((g, 128, n, 4), np.uint8)
        nib[..., 0::2] = words & 0xF
        nib[..., 1::2] = words >> 4
        vals = E2M1[nib]
    vals = vals * np.repeat(np.exp2(scales.astype(np.float64) - 127.0), 8, axis=1)[..., None]
    return vals.transpose(0, 1, 3, 2).reshape(g * 512, n)


def sigmoid(v):
    return 1.0 / (1.0 + np.exp(-np.maximum(v, -700.0)))


K, T, E, H, N = 512, 1024, 2, 1024, 128
COUNTS = (640, 384)
STARTS = np.cumsum((0,) + COUNTS)


def by_expert(wq, xq):
    return np.concatenate([wq[e].T @ xq[:, STARTS[e]:STARTS[e + 1]] for e in range(E)], axis=1)


def setup_inputs():
    n = np.random.standard_normal
    s = mx_kscale(K)[:, None]
    u = mx_kscale(H)
    expert = np.random.permutation(np.repeat(np.arange(E), COUNTS))
    slot_token = np.argsort(expert, kind="stable")
    w1 = [pack_weight(m, "e2m1") for m in n((E, K, H)) / np.sqrt(K) / s[None]]
    w3 = [pack_weight(m, "e2m1") for m in n((E, K, H)) / np.sqrt(K) / s[None] * u[None, None, :]]
    w2 = [pack_weight(m, "e2m1") for m in n((E, H, N)) / np.sqrt(H) / u[None, :, None]]
    return {
        "xT": (n((K, T)) * s).astype(np.float32),
        "w1_words": np.stack([m[0] for m in w1]),
        "w1_scales": np.stack([m[1] for m in w1]),
        "w3_words": np.stack([m[0] for m in w3]),
        "w3_scales": np.stack([m[1] for m in w3]),
        "w2_words": np.stack([m[0] for m in w2]),
        "w2_scales": np.stack([m[1] for m in w2]),
        "gate": np.tile(np.random.uniform(0.2, 1.0, T), (N, 1)).astype(np.float32),
        "offs": striped(slot_token),
    }


def reference(xT, w1_words, w1_scales, w3_words, w3_scales, w2_words, w2_scales, gate, offs):
    idx = unstriped(offs)
    w1 = np.stack([unpack_weight(w1_words[e], w1_scales[e], "e2m1") for e in range(E)])
    w3 = np.stack([unpack_weight(w3_words[e], w3_scales[e], "e2m1") for e in range(E)])
    w2 = np.stack([unpack_weight(w2_words[e], w2_scales[e], "e2m1") for e in range(E)])
    xq = mxq(f64(xT)[:, idx], 0, "e4m3")
    h = sigmoid(by_expert(w1, xq))
    h = h * by_expert(w3, xq)
    y = by_expert(w2, mxq(h, 0, "e4m3"))
    out = np.zeros((N, T))
    out[:, idx] = f64(gate) * y
    return out

@@ -1,0 +1,204 @@
+from contextlib import ExitStack
+
+import concourse.mybir as mybir
+from concourse.masks import make_identity
+
+K, T, E, H, N = 512, 1024, 2, 1024, 128
+COUNTS = (640, 384)
+FLOPS = 2 * T * (2 * K * H + H * N)
+
+P = 128
+F32 = mybir.dt.float32
+BF16 = mybir.dt.bfloat16
+I32 = mybir.dt.int32
+U32 = mybir.dt.uint32
+U16 = mybir.dt.uint16
+U8 = mybir.dt.uint8
+FP8X4 = mybir.dt.float8_e4m3fn_x4
+FP4X4 = mybir.dt.float4_e2m1fn_x4
+MULT = mybir.AluOpType.mult
+SIGMOID = mybir.ActivationFunctionType.Sigmoid
+
+HALF = 512
+GROUPS = H // HALF
+BLOCKS = T // P
+X_CHUNKS = ((0, 512), (512, 768), (768, 1024))
+SCALAR_SHARE = 3
+GATHERS = ((0, 128), (128, 384), (384, 640), (640, 896), (896, 1024))
+SCATTERS = ((0, 2), (2, 4), (4, 5), (5, 7), (7, 8))
+
+
+def tile_moe_rag_glu_sigmoid_kernel(
+    tc, xT, w1_words, w1_scales, w3_words, w3_scales, w2_words, w2_scales, gate, offs, out
+):
+    nc = tc.nc
+    with ExitStack() as ctx:
+        keep = ctx.enter_context(tc.tile_pool(name="keep", bufs=1))
+        work = ctx.enter_context(tc.tile_pool(name="work", bufs=3))
+        psum_ab = ctx.enter_context(tc.psum_pool(name="psum_ab", bufs=3))
+        psum_ty = ctx.enter_context(tc.psum_pool(name="psum_ty", bufs=1))
+
+        x_bytes = keep.tile([P, T], U8, name="x_bytes", align_bytes=64)
+        nc.gpsimd.memset(x_bytes[:], 0)
+
+        def scale_plane(name, scales, passes, width, queue):
+            plane = keep.tile([P, passes, width], U8, name=name, align_bytes=64)
+            nc.vector.memset(plane[:].rearrange("p s i -> p (s i)").bitcast(I32), 0)
+            rows = scales.rearrange("e s (a r) i -> r a (e s) i", r=4)
+            for r in range(4):
+                queue.dma_start(out=plane[r:P:32].bitcast(I32), in_=rows[r].bitcast(I32))
+            return plane
+
+        w3_plane = scale_plane("w3s", w3_scales, E, H, nc.scalar)
+        w1_plane = scale_plane("w1s", w1_scales, E, H, nc.gpsimd)
+
+        x_rows = xT.rearrange("(p j) w -> p j w", j=4)
+        x_raw = []
+        for c0, c1 in X_CHUNKS:
+            raw = keep.tile([P, 4, c1 - c0], F32, name="raw%d" % c0)
+            nc.sync.dma_start(out=raw[:], in_=x_rows[:, :, c0:c1])
+            x_raw.append(raw)
+        offsets = keep.tile([P, T // 16], U16, name="offsets")
+        nc.sync.dma_start(offsets[:], offs)
+
+        warm = keep.tile([P, 1], F32, name="warm")
+        nc.vector.memset(warm[:], 0.0)
+        nc.scalar.activation(warm[:], warm[:], SIGMOID)
+
+        w1_sb, w3_sb = [], []
+        w2_sb = keep.tile([P, E * GROUPS, 2 * N], U8, name="w2_sb", align_bytes=64)
+        gate_sb = keep.tile([P, T], F32, name="gate_sb")
+        for e in range(E):
+            for dst, src, name in ((w1_sb, w1_words, "w1_%d"), (w3_sb, w3_words, "w3_%d")):
+                words = keep.tile([P, 2 * H], U8, name=name % e, align_bytes=64)
+                nc.sync.dma_start(out=words[:].bitcast(I32), in_=src[e, 0].bitcast(I32))
+                dst.append(words)
+            if e == 0:
+                nc.sync.dma_start(
+                    out=w2_sb[:].bitcast(I32), in_=w2_words.rearrange("e s p n -> p (e s) n").bitcast(I32)
+                )
+                nc.sync.dma_start(out=gate_sb[:], in_=gate)
+        w2_plane = scale_plane("w2s", w2_scales, E * GROUPS, N, nc.gpsimd)
+
+        identity = keep.tile([P, P], F32, name="identity")
+        make_identity(nc, identity[:])
+
+        x_words = keep.tile([P, T], U32, name="x_words", align_bytes=64)
+        for raw, (c0, c1) in zip(x_raw, X_CHUNKS):
+            width = c1 - c0
+            cut = width - width * SCALAR_SHARE // 8
+            side = keep.tile([P, width, 4], BF16, name="side%d" % c0, align_bytes=64)
+            view = raw[:].rearrange("p j w -> p w j")
+            nc.vector.tensor_copy(out=side[:, :cut, :], in_=view[:, :cut, :])
+            nc.scalar.copy(out=side[:, cut:, :], in_=view[:, cut:, :])
+            nc.vector.quantize_mx(
+                out=x_words[:, c0:c1].bitcast(FP8X4),
+                scales=x_bytes[:, c0:c1],
+                in_=side[:].rearrange("p w j -> p (w j)"),
+            )
+
+        slot_words, slot_bytes = {}, {}
+
+        def gather(g):
+            s0, s1 = GATHERS[g]
+            listed = offsets[:, s0 // 16 : s1 // 16]
+            words = keep.tile([P, s1 - s0], U32, name="slot_words%d" % g, align_bytes=64)
+            nc.vector.tensor_copy(words[:], x_words[:].indirect(listed))
+            scale = keep.tile([P, s1 - s0], U8, name="slot_bytes%d" % g, align_bytes=64)
+            nc.vector.tensor_copy(scale[:], x_bytes[:].indirect(listed))
+            for s in range(s0, s1, P):
+                slot_words[s // P] = words[:, s - s0 : s - s0 + P]
+                slot_bytes[s // P] = scale[:, s - s0 : s - s0 + P]
+
+        hidden, h_codes, h_bytes, y_banks = {}, {}, {}, {}
+
+        def first_layer(b):
+            e = 0 if b * P < COUNTS[0] else 1
+            h_rows = work.tile([P, GROUPS, HALF], BF16, name="h_rows", align_bytes=64)
+            for g in range(GROUPS):
+                banks = []
+                for words, plane, tag in ((w1_sb[e], w1_plane, "a"), (w3_sb[e], w3_plane, "b")):
+                    bank = psum_ab.tile([P, HALF], F32, name=tag)
+                    nc.tensor.matmul_mx(
+                        out=bank[:],
+                        lhsT=slot_words[b].bitcast(FP8X4),
+                        lhsT_scale=slot_bytes[b],
+                        rhs=words[:, 2 * HALF * g : 2 * HALF * (g + 1)].bitcast(FP4X4),
+                        rhs_scale=plane[:, e, HALF * g : HALF * (g + 1)],
+                        start=True,
+                        stop=True,
+                    )
+                    banks.append(bank[:].rearrange("s (p u d) -> s u p d", u=2, d=2))
+                gated = work.tile([P, HALF], F32, name="gated")
+                gated_view = gated[:].rearrange("s (u p d) -> s u p d", u=2, d=2)
+                nc.scalar.activation(gated_view, banks[0], SIGMOID)
+                nc.vector.tensor_tensor(
+                    h_rows[:, g, :].rearrange("s (u p d) -> s u p d", u=2, d=2), banks[1], gated_view, MULT
+                )
+            hidden[b] = h_rows
+
+        def turn(b):
+            words = hidden[b][:].rearrange("s g c -> s (g c)").bitcast(F32)
+            turned = psum_ty.tile([P, GROUPS, 2, P], F32, name="turned")
+            for g in range(GROUPS):
+                for u in range(2):
+                    at = (2 * g + u) * P
+                    nc.tensor.transpose(turned[:, g, u, :], words[:, at : at + P], identity[:])
+            quads = work.tile([P, GROUPS * P * 4], BF16, name="quads", align_bytes=64)
+            nc.scalar.copy(
+                out=quads[:].bitcast(F32).rearrange("p (g s u) -> p g s u", g=GROUPS, u=2),
+                in_=turned[:].rearrange("p g u s -> p g s u"),
+            )
+            codes = work.tile([P, GROUPS, P], U32, name="codes", align_bytes=64)
+            scale = work.tile([P, GROUPS, P], U8, name="scale", align_bytes=64)
+            nc.vector.quantize_mx(
+                out=codes[:].rearrange("p g s -> p (g s)").bitcast(FP8X4),
+                scales=scale[:].rearrange("p g s -> p (g s)"),
+                in_=quads[:],
+            )
+            h_codes[b], h_bytes[b] = codes, scale
+
+        outT = keep.tile([P, T], F32, name="outT")
+
+        def second_layer(b):
+            e = 0 if b * P < COUNTS[0] else 1
+            first, last = [s for s in SCATTERS if s[0] <= b < s[1]][0]
+            if b == first:
+                y_banks[first] = psum_ty.tile([P, 2 * P], F32, name="y")
+            y = y_banks[first]
+            for g in range(GROUPS):
+                nc.tensor.matmul_mx(
+                    out=y[:, (b - first) * P : (b - first + 1) * P],
+                    lhsT=w2_sb[:, e * GROUPS + g, :].bitcast(FP4X4),
+                    lhsT_scale=w2_plane[:, e * GROUPS + g, :],
+                    rhs=h_codes[b][:, g, :].bitcast(FP8X4),
+                    rhs_scale=h_bytes[b][:, g, :],
+                    start=(g == 0),
+                    stop=(g == GROUPS - 1),
+                )
+            if b == last - 1:
+                width = (last - first) * P
+                weighted = work.tile([P, width], F32, name="weighted%d" % width)
+                nc.vector.tensor_tensor(
+                    weighted[:], y[:, :width], gate_sb[:, first * P : last * P], MULT
+                )
+                listed = offsets[:, first * P // 16 : last * P // 16]
+                nc.vector.tensor_copy(outT[:].indirect(listed), weighted[:])
+
+        gather(0)
+        first_layer(0)
+        gather(1)
+        first_layer(1)
+        turn(0)
+        gather(2)
+        for b in range(2, BLOCKS + 2):
+            if b == 4:
+                gather(3)
+            if b == 6:
+                gather(4)
+            if b < BLOCKS:
+                first_layer(b)
+            if b - 1 < BLOCKS:
+                turn(b - 1)
+            second_layer(b - 2)
+        nc.sync.dma_start(out=out, in_=outT[:])

@@ -49,9 +49,13 @@ def tile_moe_rag_glu_sigmoid_kernel(
                 queue.dma_start(out=plane[r:P:32].bitcast(I32), in_=rows[r].bitcast(I32))
             return plane
 
-        w3_plane = scale_plane("w3s", w3_scales, E, H, nc.scalar)
-        w1_plane = scale_plane("w1s", w1_scales, E, H, nc.gpsimd)
+        identity = keep.tile([P, P], F32, name="identity")
+        make_identity(nc, identity[:])
+        warm = keep.tile([P, 1], F32, name="warm")
+        nc.vector.memset(warm[:], 0.0)
+        nc.scalar.activation(warm[:], warm[:], SIGMOID)
 
+        w1_plane = scale_plane("w1s", w1_scales, E, H, nc.scalar)
         x_rows = xT.rearrange("(p j) w -> p j w", j=4)
         x_raw = []
         for c0, c1 in X_CHUNKS:
@@ -60,28 +64,22 @@ def tile_moe_rag_glu_sigmoid_kernel(
             x_raw.append(raw)
         offsets = keep.tile([P, T // 16], U16, name="offsets")
         nc.sync.dma_start(offsets[:], offs)
-
-        warm = keep.tile([P, 1], F32, name="warm")
-        nc.vector.memset(warm[:], 0.0)
-        nc.scalar.activation(warm[:], warm[:], SIGMOID)
+        w3_plane = scale_plane("w3s", w3_scales, E, H, nc.sync)
 
         w1_sb, w3_sb = [], []
-        w2_sb = keep.tile([P, E * GROUPS, 2 * N], U8, name="w2_sb", align_bytes=64)
         gate_sb = keep.tile([P, T], F32, name="gate_sb")
+        w2_sb = keep.tile([P, E * GROUPS, 2 * N], U8, name="w2_sb", align_bytes=64)
         for e in range(E):
             for dst, src, name in ((w1_sb, w1_words, "w1_%d"), (w3_sb, w3_words, "w3_%d")):
                 words = keep.tile([P, 2 * H], U8, name=name % e, align_bytes=64)
                 nc.sync.dma_start(out=words[:].bitcast(I32), in_=src[e, 0].bitcast(I32))
                 dst.append(words)
             if e == 0:
+                w2_plane = scale_plane("w2s", w2_scales, E * GROUPS, N, nc.sync)
                 nc.sync.dma_start(
                     out=w2_sb[:].bitcast(I32), in_=w2_words.rearrange("e s p n -> p (e s) n").bitcast(I32)
                 )
                 nc.sync.dma_start(out=gate_sb[:], in_=gate)
-        w2_plane = scale_plane("w2s", w2_scales, E * GROUPS, N, nc.gpsimd)
-
-        identity = keep.tile([P, P], F32, name="identity")
-        make_identity(nc, identity[:])
 
         x_words = keep.tile([P, T], U32, name="x_words", align_bytes=64)
         for raw, (c0, c1) in zip(x_raw, X_CHUNKS):
@@ -178,12 +176,12 @@ def tile_moe_rag_glu_sigmoid_kernel(
                 )
             if b == last - 1:
                 width = (last - first) * P
-                weighted = work.tile([P, width], F32, name="weighted%d" % width)
-                nc.vector.tensor_tensor(
-                    weighted[:], y[:, :width], gate_sb[:, first * P : last * P], MULT
-                )
+                results = work.tile([P, width], F32, name="results%d" % width)
+                nc.scalar.copy(out=results[:], in_=y[:, :width])
                 listed = offsets[:, first * P // 16 : last * P // 16]
-                nc.vector.tensor_copy(outT[:].indirect(listed), weighted[:])
+                nc.vector.tensor_tensor(
+                    outT[:].indirect(listed), results[:], gate_sb[:, first * P : last * P], MULT
+                )
 
         gather(0)
         first_layer(0)

from contextlib import ExitStack

import concourse.mybir as mybir
from concourse.masks import make_identity

K, T, E, H, N = 512, 1024, 2, 1024, 128
COUNTS = (640, 384)
FLOPS = 2 * T * (2 * K * H + H * N)

P = 128
F32 = mybir.dt.float32
BF16 = mybir.dt.bfloat16
I32 = mybir.dt.int32
U32 = mybir.dt.uint32
U16 = mybir.dt.uint16
U8 = mybir.dt.uint8
FP8X4 = mybir.dt.float8_e4m3fn_x4
FP4X4 = mybir.dt.float4_e2m1fn_x4
MULT = mybir.AluOpType.mult
SIGMOID = mybir.ActivationFunctionType.Sigmoid

HALF = 512
GROUPS = H // HALF
BLOCKS = T // P
X_CHUNKS = ((0, 512), (512, 768), (768, 1024))
SCALAR_SHARE = 3
GATHERS = ((0, 128), (128, 384), (384, 640), (640, 896), (896, 1024))
SCATTERS = ((0, 2), (2, 4), (4, 5), (5, 7), (7, 8))


def tile_moe_rag_glu_sigmoid_kernel(
    tc, xT, w1_words, w1_scales, w3_words, w3_scales, w2_words, w2_scales, gate, offs, out
):
    nc = tc.nc
    with ExitStack() as ctx:
        keep = ctx.enter_context(tc.tile_pool(name="keep", bufs=1))
        work = ctx.enter_context(tc.tile_pool(name="work", bufs=3))
        psum_ab = ctx.enter_context(tc.psum_pool(name="psum_ab", bufs=3))
        psum_ty = ctx.enter_context(tc.psum_pool(name="psum_ty", bufs=1))

        x_bytes = keep.tile([P, T], U8, name="x_bytes", align_bytes=64)
        nc.gpsimd.memset(x_bytes[:], 0)

        def scale_plane(name, scales, passes, width, queue):
            plane = keep.tile([P, passes, width], U8, name=name, align_bytes=64)
            nc.vector.memset(plane[:].rearrange("p s i -> p (s i)").bitcast(I32), 0)
            rows = scales.rearrange("e s (a r) i -> r a (e s) i", r=4)
            for r in range(4):
                queue.dma_start(out=plane[r:P:32].bitcast(I32), in_=rows[r].bitcast(I32))
            return plane

        identity = keep.tile([P, P], F32, name="identity")
        make_identity(nc, identity[:])
        warm = keep.tile([P, 1], F32, name="warm")
        nc.vector.memset(warm[:], 0.0)
        nc.scalar.activation(warm[:], warm[:], SIGMOID)

        w1_plane = scale_plane("w1s", w1_scales, E, H, nc.scalar)
        x_rows = xT.rearrange("(p j) w -> p j w", j=4)
        x_raw = []
        for c0, c1 in X_CHUNKS:
            raw = keep.tile([P, 4, c1 - c0], F32, name="raw%d" % c0)
            nc.sync.dma_start(out=raw[:], in_=x_rows[:, :, c0:c1])
            x_raw.append(raw)
        offsets = keep.tile([P, T // 16], U16, name="offsets")
        nc.sync.dma_start(offsets[:], offs)
        w3_plane = scale_plane("w3s", w3_scales, E, H, nc.sync)

        w1_sb, w3_sb = [], []
        gate_sb = keep.tile([P, T], F32, name="gate_sb")
        w2_sb = keep.tile([P, E * GROUPS, 2 * N], U8, name="w2_sb", align_bytes=64)
        for e in range(E):
            for dst, src, name in ((w1_sb, w1_words, "w1_%d"), (w3_sb, w3_words, "w3_%d")):
                words = keep.tile([P, 2 * H], U8, name=name % e, align_bytes=64)
                nc.sync.dma_start(out=words[:].bitcast(I32), in_=src[e, 0].bitcast(I32))
                dst.append(words)
            if e == 0:
                w2_plane = scale_plane("w2s", w2_scales, E * GROUPS, N, nc.sync)
                nc.sync.dma_start(
                    out=w2_sb[:].bitcast(I32), in_=w2_words.rearrange("e s p n -> p (e s) n").bitcast(I32)
                )
                nc.sync.dma_start(out=gate_sb[:], in_=gate)

        x_words = keep.tile([P, T], U32, name="x_words", align_bytes=64)
        for raw, (c0, c1) in zip(x_raw, X_CHUNKS):
            width = c1 - c0
            cut = width - width * SCALAR_SHARE // 8
            side = keep.tile([P, width, 4], BF16, name="side%d" % c0, align_bytes=64)
            view = raw[:].rearrange("p j w -> p w j")
            nc.vector.tensor_copy(out=side[:, :cut, :], in_=view[:, :cut, :])
            nc.scalar.copy(out=side[:, cut:, :], in_=view[:, cut:, :])
            nc.vector.quantize_mx(
                out=x_words[:, c0:c1].bitcast(FP8X4),
                scales=x_bytes[:, c0:c1],
                in_=side[:].rearrange("p w j -> p (w j)"),
            )

        slot_words, slot_bytes = {}, {}

        def gather(g):
            s0, s1 = GATHERS[g]
            listed = offsets[:, s0 // 16 : s1 // 16]
            words = keep.tile([P, s1 - s0], U32, name="slot_words%d" % g, align_bytes=64)
            nc.vector.tensor_copy(words[:], x_words[:].indirect(listed))
            scale = keep.tile([P, s1 - s0], U8, name="slot_bytes%d" % g, align_bytes=64)
            nc.vector.tensor_copy(scale[:], x_bytes[:].indirect(listed))
            for s in range(s0, s1, P):
                slot_words[s // P] = words[:, s - s0 : s - s0 + P]
                slot_bytes[s // P] = scale[:, s - s0 : s - s0 + P]

        hidden, h_codes, h_bytes, y_banks = {}, {}, {}, {}

        def first_layer(b):
            e = 0 if b * P < COUNTS[0] else 1
            h_rows = work.tile([P, GROUPS, HALF], BF16, name="h_rows", align_bytes=64)
            for g in range(GROUPS):
                banks = []
                for words, plane, tag in ((w1_sb[e], w1_plane, "a"), (w3_sb[e], w3_plane, "b")):
                    bank = psum_ab.tile([P, HALF], F32, name=tag)
                    nc.tensor.matmul_mx(
                        out=bank[:],
                        lhsT=slot_words[b].bitcast(FP8X4),
                        lhsT_scale=slot_bytes[b],
                        rhs=words[:, 2 * HALF * g : 2 * HALF * (g + 1)].bitcast(FP4X4),
                        rhs_scale=plane[:, e, HALF * g : HALF * (g + 1)],
                        start=True,
                        stop=True,
                    )
                    banks.append(bank[:].rearrange("s (p u d) -> s u p d", u=2, d=2))
                gated = work.tile([P, HALF], F32, name="gated")
                gated_view = gated[:].rearrange("s (u p d) -> s u p d", u=2, d=2)
                nc.scalar.activation(gated_view, banks[0], SIGMOID)
                nc.vector.tensor_tensor(
                    h_rows[:, g, :].rearrange("s (u p d) -> s u p d", u=2, d=2), banks[1], gated_view, MULT
                )
            hidden[b] = h_rows

        def turn(b):
            words = hidden[b][:].rearrange("s g c -> s (g c)").bitcast(F32)
            turned = psum_ty.tile([P, GROUPS, 2, P], F32, name="turned")
            for g in range(GROUPS):
                for u in range(2):
                    at = (2 * g + u) * P
                    nc.tensor.transpose(turned[:, g, u, :], words[:, at : at + P], identity[:])
            quads = work.tile([P, GROUPS * P * 4], BF16, name="quads", align_bytes=64)
            nc.scalar.copy(
                out=quads[:].bitcast(F32).rearrange("p (g s u) -> p g s u", g=GROUPS, u=2),
                in_=turned[:].rearrange("p g u s -> p g s u"),
            )
            codes = work.tile([P, GROUPS, P], U32, name="codes", align_bytes=64)
            scale = work.tile([P, GROUPS, P], U8, name="scale", align_bytes=64)
            nc.vector.quantize_mx(
                out=codes[:].rearrange("p g s -> p (g s)").bitcast(FP8X4),
                scales=scale[:].rearrange("p g s -> p (g s)"),
                in_=quads[:],
            )
            h_codes[b], h_bytes[b] = codes, scale

        outT = keep.tile([P, T], F32, name="outT")

        def second_layer(b):
            e = 0 if b * P < COUNTS[0] else 1
            first, last = [s for s in SCATTERS if s[0] <= b < s[1]][0]
            if b == first:
                y_banks[first] = psum_ty.tile([P, 2 * P], F32, name="y")
            y = y_banks[first]
            for g in range(GROUPS):
                nc.tensor.matmul_mx(
                    out=y[:, (b - first) * P : (b - first + 1) * P],
                    lhsT=w2_sb[:, e * GROUPS + g, :].bitcast(FP4X4),
                    lhsT_scale=w2_plane[:, e * GROUPS + g, :],
                    rhs=h_codes[b][:, g, :].bitcast(FP8X4),
                    rhs_scale=h_bytes[b][:, g, :],
                    start=(g == 0),
                    stop=(g == GROUPS - 1),
                )
            if b == last - 1:
                width = (last - first) * P
                results = work.tile([P, width], F32, name="results%d" % width)
                nc.scalar.copy(out=results[:], in_=y[:, :width])
                listed = offsets[:, first * P // 16 : last * P // 16]
                nc.vector.tensor_tensor(
                    outT[:].indirect(listed), results[:], gate_sb[:, first * P : last * P], MULT
                )

        gather(0)
        first_layer(0)
        gather(1)
        first_layer(1)
        turn(0)
        gather(2)
        for b in range(2, BLOCKS + 2):
            if b == 4:
                gather(3)
            if b == 6:
                gather(4)
            if b < BLOCKS:
                first_layer(b)
            if b - 1 < BLOCKS:
                turn(b - 1)
            second_layer(b - 2)
        nc.sync.dma_start(out=out, in_=outT[:])
